import numpy as np
import ml_dtypes


def mxq(x, axis, fmt="e4m3"):
    dtype, down = {"e4m3": (ml_dtypes.float8_e4m3fn, 7), "e5m2": (ml_dtypes.float8_e5m2, 14)}[fmt]
    v = np.moveaxis(np.asarray(x, np.float32).astype(ml_dtypes.bfloat16).astype(np.float64), axis, -1)
    blocks = v.reshape(v.shape[:-1] + (-1, 32))
    amax = np.abs(blocks).max(-1, keepdims=True)
    byte = np.maximum(np.where(amax > 0, np.frexp(amax)[1] - 1 + 127, 0) - down, 1)
    scale = np.exp2(byte - 127.0)
    codes = (blocks / scale).astype(np.float32).astype(dtype).astype(np.float64)
    return np.moveaxis((codes * scale).reshape(v.shape), -1, axis)


WIDE = False


def mx_kscale(k):
    if not WIDE:
        return np.ones(k)
    levels = np.array([10, -10, 5, -5, 0])
    if k % 512:
        return np.exp2(np.random.permutation(np.resize(levels, k // 32))).repeat(32)
    a = np.empty((k // 512, 16))
    for p in range(k // 512):
        a[p, :8] = np.random.permutation(np.resize(levels, 8))
        for g in range(8):
            far = levels[np.abs(levels - a[p, g]) >= 10]
            a[p, g + 8] = far[np.random.randint(len(far))]
    return np.exp2(a.ravel()).repeat(32)


def f64(x):
    return np.asarray(x).astype(np.float64)


def striped(idx):
    return np.tile(idx.reshape(-1, 16).T, (8, 1)).astype(np.uint16)


def unstriped(offs):
    return offs[:16].T.reshape(-1).astype(np.int64)


def pack_weight(w):
    k, n = w.shape
    w = f64(np.asarray(w, np.float32).astype(ml_dtypes.bfloat16)).reshape(k // 32, 32, n)
    amax = np.abs(w).max(1)
    byte = np.clip(np.where(amax > 0, np.frexp(amax)[1] - 1 + 127 - 7, 1), 1, 254)
    scaled = (w * np.exp2(127.0 - byte)[:, None, :]).reshape(k, n).astype(np.float32)
    words = np.ascontiguousarray(scaled.reshape(k // 512, 128, 4, n).transpose(0, 1, 3, 2)).astype(ml_dtypes.float8_e4m3fn).view(np.uint8)
    return words, np.ascontiguousarray(byte.astype(np.uint8).reshape(k // 512, 16, n))


def unpack_weight(words, scales):
    g, p, n, _ = words.shape
    vals = np.ascontiguousarray(words).view(ml_dtypes.float8_e4m3fn).astype(np.float64) * np.repeat(np.exp2(scales.astype(np.float64) - 127.0), 8, axis=1)[..., None]
    return vals.transpose(0, 1, 3, 2).reshape(g * 512, n)


K, T, D, S, V, N = 2048, 1024, 4, 512, 256, 128


def setup_inputs():
    n = np.random.standard_normal
    s = mx_kscale(K)[:, None]
    words, scales = pack_weight(n((K, N)) / np.sqrt(K) / s)
    return {
        "xT": (n((K, T)) * s).astype(np.float32),
        "w_words": words,
        "w_scales": scales,
        "gate": np.tile(np.random.uniform(0.2, 1.0, (D, 1, V)) / np.sqrt(D), (1, N, 1)).astype(np.float32),
        "offs": striped(np.random.permutation(T)[:S]),
        "pos1": striped(np.random.permutation(S)[:V]),
        "pos2": striped(np.random.permutation(S)[:V]),
        "pos3": striped(np.random.permutation(S)[:V]),
        "pos4": striped(np.random.permutation(S)[:V]),
    }


def reference(xT, w_words, w_scales, gate, offs, pos1, pos2, pos3, pos4):
    w = unpack_weight(w_words, w_scales)
    idx = unstriped(offs)
    xq = mxq(f64(xT)[:, idx], 0, "e4m3")
    y = w.T @ xq
    return sum(f64(gate[d]) * y[:, unstriped(p)] for d, p in enumerate((pos1, pos2, pos3, pos4)))

@@ -1,0 +1,127 @@
+from contextlib import ExitStack
+
+import concourse.mybir as mybir
+
+K, T, S, V, D, M = 2048, 1024, 512, 256, 4, 128
+FLOPS = 2 * K * M * S
+
+F32 = mybir.dt.float32
+BF16 = mybir.dt.bfloat16
+U32 = mybir.dt.uint32
+I32 = mybir.dt.int32
+U16 = mybir.dt.uint16
+U8 = mybir.dt.uint8
+FP8X4 = mybir.dt.float8_e4m3fn_x4
+COPY = mybir.ActivationFunctionType.Copy
+MULT = mybir.AluOpType.mult
+ADD = mybir.AluOpType.add
+
+P = 128
+PASSES = K // 512
+H = S // 2
+
+
+def tile_picked_sub_lin_none_sub_e_kernel(tc, xT, w_words, w_scales, gate, offs, pos1, pos2, pos3, pos4, out):
+    nc = tc.nc
+    with ExitStack() as ctx:
+        keep = ctx.enter_context(tc.tile_pool(name="keep", bufs=1))
+        psum = ctx.enter_context(tc.psum_pool(name="psum", bufs=1))
+
+        offs_t = keep.tile([P, S // 16], U16, name="offs_t")
+        pos_t = [keep.tile([P, V // 16], U16, name=f"pos_t{d}") for d in range(D)]
+        w_t = keep.tile([P, PASSES, M], I32, name="w_t", align_bytes=64)
+        ws_t = keep.tile([P, M], U8, name="ws_t", align_bytes=64)
+        gate_t = keep.tile([P, D, V], F32, name="gate_t")
+        y_t = keep.tile([P, S], F32, name="y_t")
+        banks = [psum.tile([P, H], F32, name=f"bank{h}") for h in range(2)]
+
+        nc.vector.memset(ws_t[:].bitcast(I32), 0)
+        nc.sync.dma_start(offs_t[:], offs)
+
+        xv = xT.rearrange("(a p u e) t -> a u p e t", p=P, u=2, e=2)
+        pieces = {c: [(0, T)] for c in range(2 * PASSES)}
+        pieces[2 * PASSES - 1] = [(0, 512), (512, 768), (768, 1024)]
+        raws = []
+        for c in range(2 * PASSES):
+            row = []
+            for i, (t0, t1) in enumerate(pieces[c]):
+                raw = keep.tile([P, 2, t1 - t0], F32, name=f"raw{c}_{i}")
+                nc.sync.dma_start(raw[:], xv[c // 2, c % 2, :, :, t0:t1])
+                row.append((t0, t1, raw))
+            raws.append(row)
+            if c == 0:
+                for q in range(4):
+                    nc.scalar.dma_start(ws_t[32 * q : 32 * q + 16, :].bitcast(I32), w_scales[:, 4 * q : 4 * q + 4, :].bitcast(I32))
+        nc.sync.dma_start(w_t[:], w_words.rearrange("a p m r -> p a (m r)").bitcast(I32))
+        for d, pos in enumerate((pos1, pos2, pos3, pos4)):
+            nc.sync.dma_start(pos_t[d][:], pos)
+        gv = gate.rearrange("d p v -> p d v")
+        nc.sync.dma_start(gate_t[:], gv)
+
+        gs = [keep.tile([P, 2 * S], U32, name=f"g{a}", align_bytes=64) for a in range(PASSES)]
+        codes = [keep.tile([P, S], U32, name=f"codes{a}", align_bytes=64) for a in range(PASSES)]
+        scales = [keep.tile([P, S], U8, name=f"scales{a}", align_bytes=64) for a in range(PASSES)]
+
+        def quantise(a, s0, s1):
+            nc.vector.quantize_mx(
+                out=codes[a][:, s0:s1].bitcast(FP8X4),
+                scales=scales[a][:, s0:s1],
+                in_=gs[a][:, 2 * s0 : 2 * s1].bitcast(BF16),
+            )
+
+        def multiply(a, h):
+            cols = slice(h * H, (h + 1) * H)
+            nc.tensor.matmul_mx(
+                out=banks[h][:],
+                lhsT=w_t[:, a, :].bitcast(FP8X4),
+                lhsT_scale=ws_t[4 * a : P, :],
+                rhs=codes[a][:, cols].bitcast(FP8X4),
+                rhs_scale=scales[a][:, cols],
+                start=(a == 0),
+                stop=(a == PASSES - 1),
+            )
+
+        pending = None
+        for c in range(2 * PASSES):
+            a, u = c // 2, c % 2
+            xb = keep.tile([P, 2 * T], BF16, name=f"xb{c}", align_bytes=64)
+            pairs = xb[:].rearrange("p (t e) -> p t e", e=2)
+            for t0, t1, raw in raws[c]:
+                n = t1 - t0
+                cut = (n * 21 // 32) // 32 * 32
+                if n == 256:
+                    cut = 96
+                src = raw[:].rearrange("p e t -> p t e")
+                nc.scalar.activation(pairs[:, t0 : t0 + cut, :], src[:, 0:cut, :], COPY)
+                nc.vector.tensor_copy(pairs[:, t0 + cut : t1, :], src[:, cut:n, :])
+            if pending is not None:
+                quantise(pending, 0, S)
+                for h in range(2):
+                    multiply(pending, h)
+                pending = None
+            g = gs[a][:].rearrange("p (s u) -> p s u", u=2)
+            if c < 2 * PASSES - 1:
+                nc.vector.tensor_copy(g[:, :, u], xb[:].bitcast(U32).indirect(offs_t[:]))
+                if u == 1:
+                    pending = a
+            else:
+                for h in range(2):
+                    nc.vector.tensor_copy(
+                        g[:, h * H : (h + 1) * H, u], xb[:].bitcast(U32).indirect(offs_t[:, h * H // 16 : (h + 1) * H // 16])
+                    )
+                for h in range(2):
+                    quantise(a, h * H, (h + 1) * H)
+                    multiply(a, h)
+
+        nc.scalar.activation(y_t[:, 0:H], banks[0][:], COPY)
+        nc.vector.tensor_copy(y_t[:, H:S], banks[1][:])
+        prods = [keep.tile([P, V], F32, name=f"prod{d}") for d in range(D)]
+        for d in range(D):
+            nc.vector.tensor_tensor(prods[d][:], y_t[:].indirect(pos_t[d][:]), gate_t[:, d, :], MULT)
+        s01 = keep.tile([P, V], F32, name="s01")
+        s012 = keep.tile([P, V], F32, name="s012")
+        total = keep.tile([P, V], F32, name="total")
+        nc.vector.tensor_tensor(s01[:], prods[0][:], prods[1][:], ADD)
+        nc.vector.tensor_tensor(s012[:], s01[:], prods[2][:], ADD)
+        nc.vector.tensor_tensor(total[:], s012[:], prods[3][:], ADD)
+        nc.sync.dma_start(out, total[:])

@@ -19,6 +19,9 @@ ADD = mybir.AluOpType.add
 P = 128
 PASSES = K // 512
 H = S // 2
+PIECES = [[[0,512],[512,1024]],[[0,1024]],[[0,1024]],[[0,1024]],[[0,1024]],[[0,1024]],[[0,1024]],[[0,512],[512,1024]]]
+CUTS = [[0.75,0.75],[0.5],[0.75],[0.7],[0.8],[0.75],[0.75],[0.95,0.75]]
+STEPPED = []
 
 
 def tile_picked_sub_lin_none_sub_e_kernel(tc, xT, w_words, w_scales, gate, offs, pos1, pos2, pos3, pos4, out):
@@ -36,37 +39,43 @@ def tile_picked_sub_lin_none_sub_e_kernel(tc, xT, w_words, w_scales, gate, offs,
         banks = [psum.tile([P, H], F32, name=f"bank{h}") for h in range(2)]
 
         nc.vector.memset(ws_t[:].bitcast(I32), 0)
-        nc.sync.dma_start(offs_t[:], offs)
 
         xv = xT.rearrange("(a p u e) t -> a u p e t", p=P, u=2, e=2)
-        pieces = {c: [(0, T)] for c in range(2 * PASSES)}
-        pieces[2 * PASSES - 1] = [(0, 512), (512, 768), (768, 1024)]
         raws = []
         for c in range(2 * PASSES):
             row = []
-            for i, (t0, t1) in enumerate(pieces[c]):
+            for i, (t0, t1) in enumerate(PIECES[c]):
                 raw = keep.tile([P, 2, t1 - t0], F32, name=f"raw{c}_{i}")
                 nc.sync.dma_start(raw[:], xv[c // 2, c % 2, :, :, t0:t1])
                 row.append((t0, t1, raw))
+                if c == 0 and i == 0:
+                    nc.sync.dma_start(offs_t[:], offs)
+                    for q in range(4):
+                        nc.scalar.dma_start(ws_t[32 * q : 32 * q + 16, :].bitcast(I32), w_scales[:, 4 * q : 4 * q + 4, :].bitcast(I32))
             raws.append(row)
-            if c == 0:
-                for q in range(4):
-                    nc.scalar.dma_start(ws_t[32 * q : 32 * q + 16, :].bitcast(I32), w_scales[:, 4 * q : 4 * q + 4, :].bitcast(I32))
-        nc.sync.dma_start(w_t[:], w_words.rearrange("a p m r -> p a (m r)").bitcast(I32))
+        wv = w_words.rearrange("a p m r -> p a (m r)").bitcast(I32)
+        for b in range(2):
+            nc.sync.dma_start(w_t[:, 2 * b : 2 * b + 2, :], wv[:, 2 * b : 2 * b + 2, :])
         for d, pos in enumerate((pos1, pos2, pos3, pos4)):
             nc.sync.dma_start(pos_t[d][:], pos)
-        gv = gate.rearrange("d p v -> p d v")
-        nc.sync.dma_start(gate_t[:], gv)
+        nc.sync.dma_start(gate_t[:], gate.rearrange("d p v -> p d v"))
 
-        gs = [keep.tile([P, 2 * S], U32, name=f"g{a}", align_bytes=64) for a in range(PASSES)]
+        grouped = [keep.tile([P, 4 * S], BF16, name=f"grouped{a}", align_bytes=64) for a in range(PASSES)]
+        pk = [keep.tile([P, 2 * S], U32, name=f"pk{a}", align_bytes=64) for a in range(PASSES)]
         codes = [keep.tile([P, S], U32, name=f"codes{a}", align_bytes=64) for a in range(PASSES)]
         scales = [keep.tile([P, S], U8, name=f"scales{a}", align_bytes=64) for a in range(PASSES)]
+
+        def interleave(copy, a, s0, s1):
+            copy(
+                grouped[a][:, 4 * s0 : 4 * s1].rearrange("p (s u e) -> p s u e", u=2, e=2),
+                pk[a][:].bitcast(BF16).rearrange("p (u s e) -> p s u e", u=2, e=2)[:, s0:s1],
+            )
 
         def quantise(a, s0, s1):
             nc.vector.quantize_mx(
                 out=codes[a][:, s0:s1].bitcast(FP8X4),
                 scales=scales[a][:, s0:s1],
-                in_=gs[a][:, 2 * s0 : 2 * s1].bitcast(BF16),
+                in_=pk[a][:, 2 * s0 : 2 * s1].bitcast(BF16) if a in STEPPED else grouped[a][:, 4 * s0 : 4 * s1],
             )
 
         def multiply(a, h):
@@ -81,35 +90,43 @@ def tile_picked_sub_lin_none_sub_e_kernel(tc, xT, w_words, w_scales, gate, offs,
                 stop=(a == PASSES - 1),
             )
 
-        pending = None
+        def gather(a, u, s0, s1, window):
+            if a in STEPPED:
+                dst = pk[a][:].rearrange("p (s u) -> p s u", u=2)[:, s0:s1, u]
+            else:
+                dst = pk[a][:, u * S + s0 : u * S + s1]
+            nc.vector.tensor_copy(dst, window.indirect(offs_t[:, s0 // 16 : s1 // 16]))
+
+        later = []
         for c in range(2 * PASSES):
             a, u = c // 2, c % 2
             xb = keep.tile([P, 2 * T], BF16, name=f"xb{c}", align_bytes=64)
             pairs = xb[:].rearrange("p (t e) -> p t e", e=2)
-            for t0, t1, raw in raws[c]:
+            for i, (t0, t1, raw) in enumerate(raws[c]):
                 n = t1 - t0
-                cut = (n * 21 // 32) // 32 * 32
-                if n == 256:
-                    cut = 96
+                cut = int(n * CUTS[c][i]) // 16 * 16
                 src = raw[:].rearrange("p e t -> p t e")
                 nc.scalar.activation(pairs[:, t0 : t0 + cut, :], src[:, 0:cut, :], COPY)
-                nc.vector.tensor_copy(pairs[:, t0 + cut : t1, :], src[:, cut:n, :])
-            if pending is not None:
-                quantise(pending, 0, S)
-                for h in range(2):
-                    multiply(pending, h)
-                pending = None
-            g = gs[a][:].rearrange("p (s u) -> p s u", u=2)
+                if cut < n:
+                    nc.vector.tensor_copy(pairs[:, t0 + cut : t1, :], src[:, cut:n, :])
+            for step in later:
+                step()
+            later = []
+            window = xb[:].bitcast(U32)
             if c < 2 * PASSES - 1:
-                nc.vector.tensor_copy(g[:, :, u], xb[:].bitcast(U32).indirect(offs_t[:]))
+                gather(a, u, 0, S, window)
                 if u == 1:
-                    pending = a
+                    if a not in STEPPED:
+                        later.append(lambda a=a: interleave(nc.vector.tensor_copy, a, 0, S))
+                    later.append(lambda a=a: quantise(a, 0, S))
+                    later.append(lambda a=a: [multiply(a, h) for h in range(2)])
             else:
                 for h in range(2):
-                    nc.vector.tensor_copy(
-                        g[:, h * H : (h + 1) * H, u], xb[:].bitcast(U32).indirect(offs_t[:, h * H // 16 : (h + 1) * H // 16])
-                    )
-                for h in range(2):
+                    gather(a, u, h * H, (h + 1) * H, window)
+                if a not in STEPPED:
+                    interleave(nc.scalar.copy, a, 0, H)
+                    interleave(nc.vector.tensor_copy, a, H, S)
+                for h in (0, 1) if a in STEPPED else (1, 0):
                     quantise(a, h * H, (h + 1) * H)
                     multiply(a, h)
 

@@ -19,8 +19,8 @@ ADD = mybir.AluOpType.add
 P = 128
 PASSES = K // 512
 H = S // 2
-PIECES = [[[0,512],[512,1024]],[[0,1024]],[[0,1024]],[[0,1024]],[[0,1024]],[[0,1024]],[[0,1024]],[[0,512],[512,1024]]]
-CUTS = [[0.75,0.75],[0.5],[0.75],[0.7],[0.8],[0.75],[0.75],[0.95,0.75]]
+PIECES = [[[0,1024]],[[0,1024]],[[0,1024]],[[0,1024]],[[0,1024]],[[0,1024]],[[0,1024]],[[0,1024]]]
+CUTS = [[0.4],[0.4],[0.7],[0.8],[0.85],[0.9],[0.95],[0.9]]
 STEPPED = []
 
 
@@ -97,7 +97,7 @@ def tile_picked_sub_lin_none_sub_e_kernel(tc, xT, w_words, w_scales, gate, offs,
                 dst = pk[a][:, u * S + s0 : u * S + s1]
             nc.vector.tensor_copy(dst, window.indirect(offs_t[:, s0 // 16 : s1 // 16]))
 
-        later = []
+        later = {}
         for c in range(2 * PASSES):
             a, u = c // 2, c % 2
             xb = keep.tile([P, 2 * T], BF16, name=f"xb{c}", align_bytes=64)
@@ -109,18 +109,19 @@ def tile_picked_sub_lin_none_sub_e_kernel(tc, xT, w_words, w_scales, gate, offs,
                 nc.scalar.activation(pairs[:, t0 : t0 + cut, :], src[:, 0:cut, :], COPY)
                 if cut < n:
                     nc.vector.tensor_copy(pairs[:, t0 + cut : t1, :], src[:, cut:n, :])
-            for step in later:
+            for step in later.pop(c, []):
                 step()
-            later = []
             window = xb[:].bitcast(U32)
             if c < 2 * PASSES - 1:
                 gather(a, u, 0, S, window)
                 if u == 1:
-                    if a not in STEPPED:
-                        later.append(lambda a=a: interleave(nc.vector.tensor_copy, a, 0, S))
-                    later.append(lambda a=a: quantise(a, 0, S))
-                    later.append(lambda a=a: [multiply(a, h) for h in range(2)])
+                    later.setdefault(c + 1, []).append(lambda a=a: interleave(nc.vector.tensor_copy, a, 0, S))
+                    later.setdefault(c + 2, []).append(lambda a=a: quantise(a, 0, S))
+                    later.setdefault(c + 2, []).append(lambda a=a: [multiply(a, h) for h in range(2)])
             else:
+                for k in sorted(later):
+                    for step in later[k]:
+                        step()
                 for h in range(2):
                     gather(a, u, h * H, (h + 1) * H, window)
                 if a not in STEPPED:
@@ -136,9 +137,12 @@ def tile_picked_sub_lin_none_sub_e_kernel(tc, xT, w_words, w_scales, gate, offs,
         for d in range(D):
             nc.vector.tensor_tensor(prods[d][:], y_t[:].indirect(pos_t[d][:]), gate_t[:, d, :], MULT)
         s01 = keep.tile([P, V], F32, name="s01")
-        s012 = keep.tile([P, V], F32, name="s012")
-        total = keep.tile([P, V], F32, name="total")
         nc.vector.tensor_tensor(s01[:], prods[0][:], prods[1][:], ADD)
-        nc.vector.tensor_tensor(s012[:], s01[:], prods[2][:], ADD)
-        nc.vector.tensor_tensor(total[:], s012[:], prods[3][:], ADD)
-        nc.sync.dma_start(out, total[:])
+        s012 = [keep.tile([P, V // 2], F32, name=f"s012_{k}") for k in range(2)]
+        total = [keep.tile([P, V // 2], F32, name=f"total_{k}") for k in range(2)]
+        cols = [slice(k * V // 2, (k + 1) * V // 2) for k in range(2)]
+        for k in range(2):
+            nc.vector.tensor_tensor(s012[k][:], s01[:, cols[k]], prods[2][:, cols[k]], ADD)
+        for k in range(2):
+            nc.vector.tensor_tensor(total[k][:], s012[k][:], prods[3][:, cols[k]], ADD)
+            nc.sync.dma_start(out[:, cols[k]], total[k][:])

@@ -20,7 +20,7 @@ P = 128
 PASSES = K // 512
 H = S // 2
 PIECES = [[[0,1024]],[[0,1024]],[[0,1024]],[[0,1024]],[[0,1024]],[[0,1024]],[[0,1024]],[[0,1024]]]
-CUTS = [[0.4],[0.4],[0.7],[0.8],[0.85],[0.9],[0.95],[0.9]]
+CUTS = [[0.3],[0.55],[0.9],[0.7],[0.8],[0.8],[0.85],[0.85]]
 STEPPED = []
 
 
@@ -97,18 +97,22 @@ def tile_picked_sub_lin_none_sub_e_kernel(tc, xT, w_words, w_scales, gate, offs,
                 dst = pk[a][:, u * S + s0 : u * S + s1]
             nc.vector.tensor_copy(dst, window.indirect(offs_t[:, s0 // 16 : s1 // 16]))
 
+        def to_bf16(dst, src):
+            nc.scalar.activation(dst, src, COPY)
+
         later = {}
         for c in range(2 * PASSES):
             a, u = c // 2, c % 2
             xb = keep.tile([P, 2 * T], BF16, name=f"xb{c}", align_bytes=64)
-            pairs = xb[:].rearrange("p (t e) -> p t e", e=2)
             for i, (t0, t1, raw) in enumerate(raws[c]):
                 n = t1 - t0
                 cut = int(n * CUTS[c][i]) // 16 * 16
-                src = raw[:].rearrange("p e t -> p t e")
-                nc.scalar.activation(pairs[:, t0 : t0 + cut, :], src[:, 0:cut, :], COPY)
-                if cut < n:
-                    nc.vector.tensor_copy(pairs[:, t0 + cut : t1, :], src[:, cut:n, :])
+                for copy, c0, c1 in ((to_bf16, 0, cut), (nc.vector.tensor_copy, cut, n)):
+                    if c1 > c0:
+                        copy(
+                            xb[:, 2 * (t0 + c0) : 2 * (t0 + c1)].rearrange("p (g i e) -> p g e i", i=4, e=2),
+                            raw[:, :, c0:c1].rearrange("p e (g i) -> p g e i", i=4),
+                        )
             for step in later.pop(c, []):
                 step()
             window = xb[:].bitcast(U32)

from contextlib import ExitStack

import concourse.mybir as mybir

K, T, S, V, D, M = 2048, 1024, 512, 256, 4, 128
FLOPS = 2 * K * M * S

F32 = mybir.dt.float32
BF16 = mybir.dt.bfloat16
U32 = mybir.dt.uint32
I32 = mybir.dt.int32
U16 = mybir.dt.uint16
U8 = mybir.dt.uint8
FP8X4 = mybir.dt.float8_e4m3fn_x4
COPY = mybir.ActivationFunctionType.Copy
MULT = mybir.AluOpType.mult
ADD = mybir.AluOpType.add

P = 128
PASSES = K // 512
H = S // 2
PIECES = [[[0,1024]],[[0,1024]],[[0,1024]],[[0,1024]],[[0,1024]],[[0,1024]],[[0,1024]],[[0,1024]]]
CUTS = [[0.3],[0.55],[0.9],[0.7],[0.8],[0.8],[0.85],[0.85]]
STEPPED = []


def tile_picked_sub_lin_none_sub_e_kernel(tc, xT, w_words, w_scales, gate, offs, pos1, pos2, pos3, pos4, out):
    nc = tc.nc
    with ExitStack() as ctx:
        keep = ctx.enter_context(tc.tile_pool(name="keep", bufs=1))
        psum = ctx.enter_context(tc.psum_pool(name="psum", bufs=1))

        offs_t = keep.tile([P, S // 16], U16, name="offs_t")
        pos_t = [keep.tile([P, V // 16], U16, name=f"pos_t{d}") for d in range(D)]
        w_t = keep.tile([P, PASSES, M], I32, name="w_t", align_bytes=64)
        ws_t = keep.tile([P, M], U8, name="ws_t", align_bytes=64)
        gate_t = keep.tile([P, D, V], F32, name="gate_t")
        y_t = keep.tile([P, S], F32, name="y_t")
        banks = [psum.tile([P, H], F32, name=f"bank{h}") for h in range(2)]

        nc.vector.memset(ws_t[:].bitcast(I32), 0)

        xv = xT.rearrange("(a p u e) t -> a u p e t", p=P, u=2, e=2)
        raws = []
        for c in range(2 * PASSES):
            row = []
            for i, (t0, t1) in enumerate(PIECES[c]):
                raw = keep.tile([P, 2, t1 - t0], F32, name=f"raw{c}_{i}")
                nc.sync.dma_start(raw[:], xv[c // 2, c % 2, :, :, t0:t1])
                row.append((t0, t1, raw))
                if c == 0 and i == 0:
                    nc.sync.dma_start(offs_t[:], offs)
                    for q in range(4):
                        nc.scalar.dma_start(ws_t[32 * q : 32 * q + 16, :].bitcast(I32), w_scales[:, 4 * q : 4 * q + 4, :].bitcast(I32))
            raws.append(row)
        wv = w_words.rearrange("a p m r -> p a (m r)").bitcast(I32)
        for b in range(2):
            nc.sync.dma_start(w_t[:, 2 * b : 2 * b + 2, :], wv[:, 2 * b : 2 * b + 2, :])
        for d, pos in enumerate((pos1, pos2, pos3, pos4)):
            nc.sync.dma_start(pos_t[d][:], pos)
        nc.sync.dma_start(gate_t[:], gate.rearrange("d p v -> p d v"))

        grouped = [keep.tile([P, 4 * S], BF16, name=f"grouped{a}", align_bytes=64) for a in range(PASSES)]
        pk = [keep.tile([P, 2 * S], U32, name=f"pk{a}", align_bytes=64) for a in range(PASSES)]
        codes = [keep.tile([P, S], U32, name=f"codes{a}", align_bytes=64) for a in range(PASSES)]
        scales = [keep.tile([P, S], U8, name=f"scales{a}", align_bytes=64) for a in range(PASSES)]

        def interleave(copy, a, s0, s1):
            copy(
                grouped[a][:, 4 * s0 : 4 * s1].rearrange("p (s u e) -> p s u e", u=2, e=2),
                pk[a][:].bitcast(BF16).rearrange("p (u s e) -> p s u e", u=2, e=2)[:, s0:s1],
            )

        def quantise(a, s0, s1):
            nc.vector.quantize_mx(
                out=codes[a][:, s0:s1].bitcast(FP8X4),
                scales=scales[a][:, s0:s1],
                in_=pk[a][:, 2 * s0 : 2 * s1].bitcast(BF16) if a in STEPPED else grouped[a][:, 4 * s0 : 4 * s1],
            )

        def multiply(a, h):
            cols = slice(h * H, (h + 1) * H)
            nc.tensor.matmul_mx(
                out=banks[h][:],
                lhsT=w_t[:, a, :].bitcast(FP8X4),
                lhsT_scale=ws_t[4 * a : P, :],
                rhs=codes[a][:, cols].bitcast(FP8X4),
                rhs_scale=scales[a][:, cols],
                start=(a == 0),
                stop=(a == PASSES - 1),
            )

        def gather(a, u, s0, s1, window):
            if a in STEPPED:
                dst = pk[a][:].rearrange("p (s u) -> p s u", u=2)[:, s0:s1, u]
            else:
                dst = pk[a][:, u * S + s0 : u * S + s1]
            nc.vector.tensor_copy(dst, window.indirect(offs_t[:, s0 // 16 : s1 // 16]))

        def to_bf16(dst, src):
            nc.scalar.activation(dst, src, COPY)

        later = {}
        for c in range(2 * PASSES):
            a, u = c // 2, c % 2
            xb = keep.tile([P, 2 * T], BF16, name=f"xb{c}", align_bytes=64)
            for i, (t0, t1, raw) in enumerate(raws[c]):
                n = t1 - t0
                cut = int(n * CUTS[c][i]) // 16 * 16
                for copy, c0, c1 in ((to_bf16, 0, cut), (nc.vector.tensor_copy, cut, n)):
                    if c1 > c0:
                        copy(
                            xb[:, 2 * (t0 + c0) : 2 * (t0 + c1)].rearrange("p (g i e) -> p g e i", i=4, e=2),
                            raw[:, :, c0:c1].rearrange("p e (g i) -> p g e i", i=4),
                        )
            for step in later.pop(c, []):
                step()
            window = xb[:].bitcast(U32)
            if c < 2 * PASSES - 1:
                gather(a, u, 0, S, window)
                if u == 1:
                    later.setdefault(c + 1, []).append(lambda a=a: interleave(nc.vector.tensor_copy, a, 0, S))
                    later.setdefault(c + 2, []).append(lambda a=a: quantise(a, 0, S))
                    later.setdefault(c + 2, []).append(lambda a=a: [multiply(a, h) for h in range(2)])
            else:
                for k in sorted(later):
                    for step in later[k]:
                        step()
                for h in range(2):
                    gather(a, u, h * H, (h + 1) * H, window)
                if a not in STEPPED:
                    interleave(nc.scalar.copy, a, 0, H)
                    interleave(nc.vector.tensor_copy, a, H, S)
                for h in (0, 1) if a in STEPPED else (1, 0):
                    quantise(a, h * H, (h + 1) * H)
                    multiply(a, h)

        nc.scalar.activation(y_t[:, 0:H], banks[0][:], COPY)
        nc.vector.tensor_copy(y_t[:, H:S], banks[1][:])
        prods = [keep.tile([P, V], F32, name=f"prod{d}") for d in range(D)]
        for d in range(D):
            nc.vector.tensor_tensor(prods[d][:], y_t[:].indirect(pos_t[d][:]), gate_t[:, d, :], MULT)
        s01 = keep.tile([P, V], F32, name="s01")
        nc.vector.tensor_tensor(s01[:], prods[0][:], prods[1][:], ADD)
        s012 = [keep.tile([P, V // 2], F32, name=f"s012_{k}") for k in range(2)]
        total = [keep.tile([P, V // 2], F32, name=f"total_{k}") for k in range(2)]
        cols = [slice(k * V // 2, (k + 1) * V // 2) for k in range(2)]
        for k in range(2):
            nc.vector.tensor_tensor(s012[k][:], s01[:, cols[k]], prods[2][:, cols[k]], ADD)
        for k in range(2):
            nc.vector.tensor_tensor(total[k][:], s012[k][:], prods[3][:, cols[k]], ADD)
            nc.sync.dma_start(out[:, cols[k]], total[k][:])
